import numpy as np
import ml_dtypes


def mxq(x, axis, fmt="e4m3"):
    dtype, down = {"e4m3": (ml_dtypes.float8_e4m3fn, 7), "e5m2": (ml_dtypes.float8_e5m2, 14)}[fmt]
    v = np.moveaxis(np.asarray(x, np.float32).astype(ml_dtypes.bfloat16).astype(np.float64), axis, -1)
    blocks = v.reshape(v.shape[:-1] + (-1, 32))
    amax = np.abs(blocks).max(-1, keepdims=True)
    byte = np.maximum(np.where(amax > 0, np.frexp(amax)[1] - 1 + 127, 0) - down, 1)
    scale = np.exp2(byte - 127.0)
    codes = (blocks / scale).astype(np.float32).astype(dtype).astype(np.float64)
    return np.moveaxis((codes * scale).reshape(v.shape), -1, axis)


WIDE = False


def mx_kscale(k):
    if not WIDE:
        return np.ones(k)
    levels = np.array([10, -10, 5, -5, 0])
    if k % 512:
        return np.exp2(np.random.permutation(np.resize(levels, k // 32))).repeat(32)
    a = np.empty((k // 512, 16))
    for p in range(k // 512):
        a[p, :8] = np.random.permutation(np.resize(levels, 8))
        for g in range(8):
            far = levels[np.abs(levels - a[p, g]) >= 10]
            a[p, g + 8] = far[np.random.randint(len(far))]
    return np.exp2(a.ravel()).repeat(32)


def f64(x):
    return np.asarray(x).astype(np.float64)


def striped(idx):
    return np.tile(idx.reshape(-1, 16).T, (8, 1)).astype(np.uint16)


def unstriped(offs):
    return offs[:16].T.reshape(-1).astype(np.int64)


E2M1 = np.array([0.0, 0.5, 1.0, 1.5, 2.0, 3.0, 4.0, 6.0, -0.0, -0.5, -1.0, -1.5, -2.0, -3.0, -4.0, -6.0])


def pack_weight(w, fmt):
    k, n = w.shape
    w = f64(np.asarray(w, np.float32).astype(ml_dtypes.bfloat16)).reshape(k // 32, 32, n)
    amax = np.abs(w).max(1)
    if fmt == "e4m3":
        byte = np.frexp(amax)[1] - 1 + 127 - 7
    else:
        mant, ex = np.frexp(amax / 6.0)
        byte = np.where(mant > 0.5, ex, ex - 1) + 127
    byte = np.clip(np.where(amax > 0, byte, 1), 1, 254)
    scaled = (w * np.exp2(127.0 - byte)[:, None, :]).reshape(k, n).astype(np.float32)
    by_word = np.ascontiguousarray(scaled.reshape(k // 512, 128, 4, n).transpose(0, 1, 3, 2))
    if fmt == "e4m3":
        words = by_word.astype(ml_dtypes.float8_e4m3fn).view(np.uint8)
    else:
        c = by_word.astype(ml_dtypes.float4_e2m1fn).view(np.uint8) & 0xF
        words = (c[..., 0::2] | (c[..., 1::2] << 4)).reshape(k // 512, 128, 2 * n)
    return np.ascontiguousarray(words), np.ascontiguousarray(byte.astype(np.uint8).reshape(k // 512, 16, n))


def unpack_weight(words, scales, fmt):
    g, _, n = scales.shape
    words = np.ascontiguousarray(words).reshape(g, 128, n, -1)
    if fmt == "e4m3":
        vals = words.view(ml_dtypes.float8_e4m3fn).astype(np.float64)
    else:
        nib = np.empty((g, 128, n, 4), np.uint8)
        nib[..., 0::2] = words & 0xF
        nib[..., 1::2] = words >> 4
        vals = E2M1[nib]
    vals = vals * np.repeat(np.exp2(scales.astype(np.float64) - 127.0), 8, axis=1)[..., None]
    return vals.transpose(0, 1, 3, 2).reshape(g * 512, n)


def pack_table(v):
    words, scales = pack_weight(v, "e4m3")
    return np.concatenate([words.reshape(words.shape[0], -1), scales.reshape(scales.shape[0], -1)], axis=1)


def unpack_table(tab):
    g, t = tab.shape[0], tab.shape[1] // 528
    return unpack_weight(tab[:, :512 * t].reshape(g, 128, t, 4), tab[:, 512 * t:].reshape(g, 16, t), "e4m3")


def gelu(v):
    return 0.5 * v * (1.0 + np.tanh(np.sqrt(2.0 / np.pi) * (v + 0.044715 * v**3)))


K, M, T, S = 512, 1024, 2048, 256


def setup_inputs():
    n = np.random.standard_normal
    s = mx_kscale(K)[:, None]
    p_w0 = pack_weight(n((K, M)) / np.sqrt(3 * K) / s, "e2m1")
    p_w1 = pack_weight(n((K, M)) / np.sqrt(3 * K) / s, "e4m3")
    return {
        "tab": pack_table(n((K, T)) * s),
        "w0_words": p_w0[0],
        "w0_scales": p_w0[1],
        "w1_words": p_w1[0],
        "w1_scales": p_w1[1],
        "w2": (n((K, M)) / np.sqrt(3 * K) / s).astype(np.float32),
        "b": (0.3 * n(1024)).astype(np.float32),
        "offs": striped(np.concatenate([np.random.permutation(T)[:S] for _ in range(3)])),
    }


def reference(tab, w0_words, w0_scales, w1_words, w1_scales, w2, b, offs):
    v = unpack_table(tab)
    idx = unstriped(offs).reshape(3, S)
    w0_ = unpack_weight(w0_words, w0_scales, "e2m1")
    w1_ = unpack_weight(w1_words, w1_scales, "e4m3")
    w2_ = mxq(f64(w2), 0, "e4m3")
    y = w0_.T @ v[:, idx[0]] + w1_.T @ v[:, idx[1]] + w2_.T @ v[:, idx[2]]
    return gelu(y + f64(b)[:, None])

@@ -1,0 +1,156 @@
+from contextlib import ExitStack
+
+import concourse.mybir as mybir
+from concourse.masks import make_identity
+
+K, M, T, S = 512, 1024, 2048, 256
+FLOPS = 2 * 3 * K * M * S
+
+F32 = mybir.dt.float32
+BF16 = mybir.dt.bfloat16
+I32 = mybir.dt.int32
+U32 = mybir.dt.uint32
+U16 = mybir.dt.uint16
+U8 = mybir.dt.uint8
+FP8X4 = mybir.dt.float8_e4m3fn_x4
+FP4X4 = mybir.dt.float4_e2m1fn_x4
+GELU = mybir.ActivationFunctionType.Gelu_apprx_tanh
+
+P = 128
+PACK = 4
+TILES = M // P
+W2_LOADS = [(0, 256), (256, 512), (512, 768), (768, 1024)]
+W2_PARTS = [(0, 256, "scalar"), (256, 512, "scalar"), (512, 768, "vector"), (768, 896, "vector"), (896, 1024, "vector")]
+STORES = [(0, 2), (2, 4), (4, 6), (6, 7), (7, 8)]
+
+
+def load_scale_rows(queue, plane, rows, first):
+    for q in range(4):
+        queue.dma_start(
+            out=plane[32 * q + first : 32 * q + first + 4, :].bitcast(I32),
+            in_=rows[4 * q : 4 * q + 4, :].bitcast(I32),
+        )
+
+
+def tile_list_tabfield_gelu_kernel(tc, tab, w0_words, w0_scales, w1_words, w1_scales, w2, b, offs, out):
+    nc = tc.nc
+    with ExitStack() as ctx:
+        keep = ctx.enter_context(tc.tile_pool(name="keep", bufs=1))
+        psum = ctx.enter_context(tc.psum_pool(name="psum", bufs=1))
+
+        offsets = keep.tile([P, 3 * S // 16], U16, name="offsets")
+        tab_words = keep.tile([P, T], I32, name="tab_words", align_bytes=64)
+        tab_plane = keep.tile([P, T], U8, name="tab_plane", align_bytes=64)
+        w0_codes = keep.tile([P, 2 * M], U8, name="w0_codes", align_bytes=64)
+        w1_codes = keep.tile([P, M], I32, name="w1_codes", align_bytes=64)
+        w0_plane = keep.tile([P, M], U8, name="w0_plane", align_bytes=64)
+        w1_plane = keep.tile([P, M], U8, name="w1_plane", align_bytes=64)
+        bias_rows = keep.tile([P, P], F32, name="bias_rows")
+        identity = keep.tile([P, P], F32, name="identity")
+        bias = keep.tile([P, TILES], F32, name="bias")
+        warm = keep.tile([P, 1], F32, name="warm")
+        warm_out = keep.tile([P, 1], F32, name="warm_out")
+        raws = [keep.tile([P, PACK, c1 - c0], F32, name="w2_raw%d" % c0) for c0, c1 in W2_LOADS]
+        w2_rows = w2.rearrange("(p i) n -> p i n", i=PACK)
+
+        def load_w2(n):
+            nc.sync.dma_start(out=raws[n][:], in_=w2_rows[:, :, W2_LOADS[n][0] : W2_LOADS[n][1]])
+
+        nc.vector.memset(tab_plane[:].bitcast(I32), 0)
+        nc.gpsimd.memset(bias_rows[:], 0.0)
+        nc.vector.memset(warm[:], 0.0)
+        nc.vector.memset(w1_plane[:].bitcast(I32), 0)
+        nc.vector.memset(w0_plane[:].bitcast(I32), 0)
+        make_identity(nc, identity[:])
+
+        nc.sync.dma_start(offsets[:], offs)
+        nc.sync.dma_start(out=tab_words[:], in_=tab[0, 0 : K * T].rearrange("(p x) -> p x", p=P).bitcast(I32))
+        load_scale_rows(nc.scalar, tab_plane, tab[0, K * T :].rearrange("(q t) -> q t", q=16), 0)
+        nc.scalar.dma_start(out=bias_rows[0:TILES, :], in_=b.rearrange("(m p) -> m p", p=P))
+        nc.scalar.activation(out=warm_out[:], in_=warm[:], func=GELU)
+        nc.sync.dma_start(out=w1_codes[:], in_=w1_words[0].rearrange("p n i -> p (n i)").bitcast(I32))
+        load_w2(0)
+        load_scale_rows(nc.sync, w1_plane, w1_scales[0], 4)
+        nc.sync.dma_start(out=w0_codes[:].bitcast(I32), in_=w0_words[0].bitcast(I32))
+        load_w2(1)
+        load_scale_rows(nc.sync, w0_plane, w0_scales[0], 0)
+        load_w2(2)
+        load_w2(3)
+
+        turned = psum.tile([P, P], F32, name="turned", tag="acc%d" % (TILES - 1))
+        nc.tensor.transpose(turned[:], bias_rows[:], identity[:])
+        nc.scalar.copy(out=bias[:], in_=turned[:, 0:TILES])
+
+        words, planes = {}, {}
+        fields = [offsets[:, f * S // 16 : (f + 1) * S // 16] for f in range(3)]
+        for kind, f in (("plane", 1), ("words", 1), ("plane", 0), ("words", 0), ("plane", 2), ("words", 2)):
+            if kind == "plane":
+                planes[f] = keep.tile([P, S], U8, name="plane%d" % f, align_bytes=64)
+                nc.vector.tensor_copy(out=planes[f][:], in_=tab_plane[:].indirect(fields[f]))
+            else:
+                words[f] = keep.tile([P, S], U32, name="words%d" % f, align_bytes=64)
+                nc.vector.tensor_copy(out=words[f][:], in_=tab_words[:].bitcast(U32).indirect(fields[f]))
+
+        accs = [psum.tile([P, S], F32, name="acc%d" % m, tag="acc%d" % m) for m in range(TILES)]
+        for m in range(TILES):
+            nc.tensor.matmul_mx(
+                out=accs[m][:],
+                lhsT=w1_codes[:, m * P : (m + 1) * P].bitcast(FP8X4),
+                lhsT_scale=w1_plane[4:P, m * P : (m + 1) * P],
+                rhs=words[1][:].bitcast(FP8X4),
+                rhs_scale=planes[1][:],
+                start=True,
+                stop=False,
+            )
+
+        w2_codes, w2_planes = {}, {}
+        grouped = []
+        for n, (c0, c1, engine) in enumerate(W2_PARTS):
+            width = c1 - c0
+            load = [x for x, (l0, l1) in enumerate(W2_LOADS) if l0 <= c0 < l1][0]
+            l0 = W2_LOADS[load][0]
+            part = keep.tile([P, width, PACK], BF16, name="grouped%d" % n, align_bytes=64)
+            dst = part[:].rearrange("p (c e) i -> p c i e", e=4)
+            src = raws[load][:, :, c0 - l0 : c1 - l0].rearrange("p i (c e) -> p c i e", e=4)
+            if engine == "scalar":
+                nc.scalar.copy(out=dst, in_=src)
+            else:
+                nc.vector.tensor_copy(out=dst, in_=src)
+            grouped.append(part)
+        for n, (c0, c1, engine) in enumerate(W2_PARTS):
+            width = c1 - c0
+            codes = keep.tile([P, width], U32, name="w2_codes%d" % n, align_bytes=64)
+            plane = keep.tile([P, width], U8, name="w2_plane%d" % n, align_bytes=64)
+            nc.vector.quantize_mx(
+                out=codes[:].bitcast(FP8X4), scales=plane[:], in_=grouped[n][:].rearrange("p c i -> p (c i)")
+            )
+            for x in range(width // P):
+                w2_codes[c0 // P + x] = codes[:, x * P : (x + 1) * P]
+                w2_planes[c0 // P + x] = plane[:, x * P : (x + 1) * P]
+
+        out_rows = out.rearrange("(m p) j -> p m j", p=P)
+        for m0, m1 in STORES:
+            result = keep.tile([P, m1 - m0, S], F32, name="result%d" % m0)
+            for m in range(m0, m1):
+                for h in range(S // P):
+                    cols = slice(h * P, (h + 1) * P)
+                    nc.tensor.matmul_mx(
+                        out=accs[m][:, cols],
+                        lhsT=w0_codes[:, 2 * m * P : 2 * (m + 1) * P].bitcast(FP4X4),
+                        lhsT_scale=w0_plane[:, m * P : (m + 1) * P],
+                        rhs=words[0][:, cols].bitcast(FP8X4),
+                        rhs_scale=planes[0][:, cols],
+                        start=False,
+                        stop=False,
+                    )
+                nc.tensor.matmul_mx(
+                    out=accs[m][:],
+                    lhsT=w2_codes[m].bitcast(FP8X4),
+                    lhsT_scale=w2_planes[m],
+                    rhs=words[2][:].bitcast(FP8X4),
+                    rhs_scale=planes[2][:],
+                    start=False,
+                    stop=True,
+                )
+                nc.scalar.activation(out=result[:, m - m0, :], in_=accs[m][:], func=GELU, bias=bias[:, m : m + 1])
+            nc.sync.dma_start(out=out_rows[:, m0:m1, :], in_=result[:])

@@ -19,17 +19,14 @@ GELU = mybir.ActivationFunctionType.Gelu_apprx_tanh
 P = 128
 PACK = 4
 TILES = M // P
-W2_LOADS = [(0, 256), (256, 512), (512, 768), (768, 1024)]
-W2_PARTS = [(0, 256, "scalar"), (256, 512, "scalar"), (512, 768, "vector"), (768, 896, "vector"), (896, 1024, "vector")]
+W2_LOADS = [(0, 640), (640, 896), (896, 1024)]
+W2_PARTS = [(0, 128, "vector"), (128, 256, "vector"), (256, 384, "vector"), (384, 640, "scalar"), (640, 768, "vector"), (768, 896, "vector"), (896, 1024, "vector")]
 STORES = [(0, 2), (2, 4), (4, 6), (6, 7), (7, 8)]
 
 
 def load_scale_rows(queue, plane, rows, first):
-    for q in range(4):
-        queue.dma_start(
-            out=plane[32 * q + first : 32 * q + first + 4, :].bitcast(I32),
-            in_=rows[4 * q : 4 * q + 4, :].bitcast(I32),
-        )
+    for r in range(4):
+        queue.dma_start(out=plane[first + r : P : 32, :].bitcast(I32), in_=rows[r:16:4, :].bitcast(I32))
 
 
 def tile_list_tabfield_gelu_kernel(tc, tab, w0_words, w0_scales, w1_words, w1_scales, w2, b, offs, out):
@@ -64,18 +61,17 @@ def tile_list_tabfield_gelu_kernel(tc, tab, w0_words, w0_scales, w1_words, w1_sc
         make_identity(nc, identity[:])
 
         nc.sync.dma_start(offsets[:], offs)
-        nc.sync.dma_start(out=tab_words[:], in_=tab[0, 0 : K * T].rearrange("(p x) -> p x", p=P).bitcast(I32))
-        load_scale_rows(nc.scalar, tab_plane, tab[0, K * T :].rearrange("(q t) -> q t", q=16), 0)
-        nc.scalar.dma_start(out=bias_rows[0:TILES, :], in_=b.rearrange("(m p) -> m p", p=P))
-        nc.scalar.activation(out=warm_out[:], in_=warm[:], func=GELU)
         nc.sync.dma_start(out=w1_codes[:], in_=w1_words[0].rearrange("p n i -> p (n i)").bitcast(I32))
-        load_w2(0)
+        load_scale_rows(nc.sync, tab_plane, tab[0, K * T :].rearrange("(q t) -> q t", q=16), 0)
+        nc.sync.dma_start(out=tab_words[:], in_=tab[0, 0 : K * T].rearrange("(p x) -> p x", p=P).bitcast(I32))
+        nc.sync.dma_start(out=bias_rows[0:TILES, :], in_=b.rearrange("(m p) -> m p", p=P))
+        nc.scalar.activation(out=warm_out[:], in_=warm[:], func=GELU)
         load_scale_rows(nc.sync, w1_plane, w1_scales[0], 4)
+        load_w2(0)
         nc.sync.dma_start(out=w0_codes[:].bitcast(I32), in_=w0_words[0].bitcast(I32))
-        load_w2(1)
         load_scale_rows(nc.sync, w0_plane, w0_scales[0], 0)
+        load_w2(1)
         load_w2(2)
-        load_w2(3)
 
         turned = psum.tile([P, P], F32, name="turned", tag="acc%d" % (TILES - 1))
         nc.tensor.transpose(turned[:], bias_rows[:], identity[:])
@@ -83,7 +79,7 @@ def tile_list_tabfield_gelu_kernel(tc, tab, w0_words, w0_scales, w1_words, w1_sc
 
         words, planes = {}, {}
         fields = [offsets[:, f * S // 16 : (f + 1) * S // 16] for f in range(3)]
-        for kind, f in (("plane", 1), ("words", 1), ("plane", 0), ("words", 0), ("plane", 2), ("words", 2)):
+        for kind, f in (("plane", 1), ("plane", 0), ("plane", 2), ("words", 1), ("words", 0), ("words", 2)):
             if kind == "plane":
                 planes[f] = keep.tile([P, S], U8, name="plane%d" % f, align_bytes=64)
                 nc.vector.tensor_copy(out=planes[f][:], in_=tab_plane[:].indirect(fields[f]))
@@ -103,30 +99,45 @@ def tile_list_tabfield_gelu_kernel(tc, tab, w0_words, w0_scales, w1_words, w1_sc
                 stop=False,
             )
 
-        w2_codes, w2_planes = {}, {}
-        grouped = []
-        for n, (c0, c1, engine) in enumerate(W2_PARTS):
-            width = c1 - c0
+        w2_codes, w2_planes, grouped = {}, {}, {}
+
+        def interleave(n):
+            c0, c1, engine = W2_PARTS[n]
             load = [x for x, (l0, l1) in enumerate(W2_LOADS) if l0 <= c0 < l1][0]
             l0 = W2_LOADS[load][0]
-            part = keep.tile([P, width, PACK], BF16, name="grouped%d" % n, align_bytes=64)
-            dst = part[:].rearrange("p (c e) i -> p c i e", e=4)
+            grouped[n] = keep.tile([P, c1 - c0, PACK], BF16, name="grouped%d" % n, align_bytes=64)
+            dst = grouped[n][:].rearrange("p (c e) i -> p c i e", e=4)
             src = raws[load][:, :, c0 - l0 : c1 - l0].rearrange("p i (c e) -> p c i e", e=4)
             if engine == "scalar":
                 nc.scalar.copy(out=dst, in_=src)
             else:
                 nc.vector.tensor_copy(out=dst, in_=src)
-            grouped.append(part)
-        for n, (c0, c1, engine) in enumerate(W2_PARTS):
-            width = c1 - c0
-            codes = keep.tile([P, width], U32, name="w2_codes%d" % n, align_bytes=64)
-            plane = keep.tile([P, width], U8, name="w2_plane%d" % n, align_bytes=64)
+
+        def quantize(n):
+            c0, c1, engine = W2_PARTS[n]
+            codes = keep.tile([P, c1 - c0], U32, name="w2_codes%d" % n, align_bytes=64)
+            plane = keep.tile([P, c1 - c0], U8, name="w2_plane%d" % n, align_bytes=64)
             nc.vector.quantize_mx(
                 out=codes[:].bitcast(FP8X4), scales=plane[:], in_=grouped[n][:].rearrange("p c i -> p (c i)")
             )
-            for x in range(width // P):
+            for x in range((c1 - c0) // P):
                 w2_codes[c0 // P + x] = codes[:, x * P : (x + 1) * P]
                 w2_planes[c0 // P + x] = plane[:, x * P : (x + 1) * P]
+
+        interleave(0)
+        interleave(3)
+        interleave(1)
+        quantize(0)
+        interleave(2)
+        quantize(1)
+        quantize(2)
+        quantize(3)
+        interleave(4)
+        interleave(5)
+        quantize(4)
+        quantize(5)
+        interleave(6)
+        quantize(6)
 
         out_rows = out.rearrange("(m p) j -> p m j", p=P)
         for m0, m1 in STORES:

@@ -19,8 +19,8 @@ GELU = mybir.ActivationFunctionType.Gelu_apprx_tanh
 P = 128
 PACK = 4
 TILES = M // P
-W2_LOADS = [(0, 640), (640, 896), (896, 1024)]
-W2_PARTS = [(0, 128, "vector"), (128, 256, "vector"), (256, 384, "vector"), (384, 640, "scalar"), (640, 768, "vector"), (768, 896, "vector"), (896, 1024, "vector")]
+W2_LOADS = [(0, 384), (384, 640), (640, 896), (896, 1024)]
+W2_PARTS = [(0, 128, "vector"), (128, 256, "vector"), (256, 384, "scalar"), (384, 512, "vector"), (512, 640, "vector"), (640, 768, "vector"), (768, 896, "vector"), (896, 1024, "vector")]
 STORES = [(0, 2), (2, 4), (4, 6), (6, 7), (7, 8)]
 
 
@@ -67,11 +67,12 @@ def tile_list_tabfield_gelu_kernel(tc, tab, w0_words, w0_scales, w1_words, w1_sc
         nc.sync.dma_start(out=bias_rows[0:TILES, :], in_=b.rearrange("(m p) -> m p", p=P))
         nc.scalar.activation(out=warm_out[:], in_=warm[:], func=GELU)
         load_scale_rows(nc.sync, w1_plane, w1_scales[0], 4)
-        load_w2(0)
         nc.sync.dma_start(out=w0_codes[:].bitcast(I32), in_=w0_words[0].bitcast(I32))
+        load_w2(0)
         load_scale_rows(nc.sync, w0_plane, w0_scales[0], 0)
         load_w2(1)
         load_w2(2)
+        load_w2(3)
 
         turned = psum.tile([P, P], F32, name="turned", tag="acc%d" % (TILES - 1))
         nc.tensor.transpose(turned[:], bias_rows[:], identity[:])
@@ -106,8 +107,8 @@ def tile_list_tabfield_gelu_kernel(tc, tab, w0_words, w0_scales, w1_words, w1_sc
             load = [x for x, (l0, l1) in enumerate(W2_LOADS) if l0 <= c0 < l1][0]
             l0 = W2_LOADS[load][0]
             grouped[n] = keep.tile([P, c1 - c0, PACK], BF16, name="grouped%d" % n, align_bytes=64)
-            dst = grouped[n][:].rearrange("p (c e) i -> p c i e", e=4)
-            src = raws[load][:, :, c0 - l0 : c1 - l0].rearrange("p i (c e) -> p c i e", e=4)
+            dst = grouped[n][:].rearrange("p (c e) i -> p c i e", e=2)
+            src = raws[load][:, :, c0 - l0 : c1 - l0].rearrange("p i (c e) -> p c i e", e=2)
             if engine == "scalar":
                 nc.scalar.copy(out=dst, in_=src)
             else:
@@ -125,19 +126,21 @@ def tile_list_tabfield_gelu_kernel(tc, tab, w0_words, w0_scales, w1_words, w1_sc
                 w2_planes[c0 // P + x] = plane[:, x * P : (x + 1) * P]
 
         interleave(0)
-        interleave(3)
+        interleave(2)
         interleave(1)
         quantize(0)
-        interleave(2)
         quantize(1)
         quantize(2)
-        quantize(3)
+        interleave(3)
         interleave(4)
-        interleave(5)
+        quantize(3)
         quantize(4)
-        quantize(5)
+        interleave(5)
         interleave(6)
+        quantize(5)
         quantize(6)
+        interleave(7)
+        quantize(7)
 
         out_rows = out.rearrange("(m p) j -> p m j", p=P)
         for m0, m1 in STORES:

from contextlib import ExitStack

import concourse.mybir as mybir
from concourse.masks import make_identity

K, M, T, S = 512, 1024, 2048, 256
FLOPS = 2 * 3 * K * M * S

F32 = mybir.dt.float32
BF16 = mybir.dt.bfloat16
I32 = mybir.dt.int32
U32 = mybir.dt.uint32
U16 = mybir.dt.uint16
U8 = mybir.dt.uint8
FP8X4 = mybir.dt.float8_e4m3fn_x4
FP4X4 = mybir.dt.float4_e2m1fn_x4
GELU = mybir.ActivationFunctionType.Gelu_apprx_tanh

P = 128
PACK = 4
TILES = M // P
W2_LOADS = [(0, 384), (384, 640), (640, 896), (896, 1024)]
W2_PARTS = [(0, 128, "vector"), (128, 256, "vector"), (256, 384, "scalar"), (384, 512, "vector"), (512, 640, "vector"), (640, 768, "vector"), (768, 896, "vector"), (896, 1024, "vector")]
STORES = [(0, 2), (2, 4), (4, 6), (6, 7), (7, 8)]


def load_scale_rows(queue, plane, rows, first):
    for r in range(4):
        queue.dma_start(out=plane[first + r : P : 32, :].bitcast(I32), in_=rows[r:16:4, :].bitcast(I32))


def tile_list_tabfield_gelu_kernel(tc, tab, w0_words, w0_scales, w1_words, w1_scales, w2, b, offs, out):
    nc = tc.nc
    with ExitStack() as ctx:
        keep = ctx.enter_context(tc.tile_pool(name="keep", bufs=1))
        psum = ctx.enter_context(tc.psum_pool(name="psum", bufs=1))

        offsets = keep.tile([P, 3 * S // 16], U16, name="offsets")
        tab_words = keep.tile([P, T], I32, name="tab_words", align_bytes=64)
        tab_plane = keep.tile([P, T], U8, name="tab_plane", align_bytes=64)
        w0_codes = keep.tile([P, 2 * M], U8, name="w0_codes", align_bytes=64)
        w1_codes = keep.tile([P, M], I32, name="w1_codes", align_bytes=64)
        w0_plane = keep.tile([P, M], U8, name="w0_plane", align_bytes=64)
        w1_plane = keep.tile([P, M], U8, name="w1_plane", align_bytes=64)
        bias_rows = keep.tile([P, P], F32, name="bias_rows")
        identity = keep.tile([P, P], F32, name="identity")
        bias = keep.tile([P, TILES], F32, name="bias")
        warm = keep.tile([P, 1], F32, name="warm")
        warm_out = keep.tile([P, 1], F32, name="warm_out")
        raws = [keep.tile([P, PACK, c1 - c0], F32, name="w2_raw%d" % c0) for c0, c1 in W2_LOADS]
        w2_rows = w2.rearrange("(p i) n -> p i n", i=PACK)

        def load_w2(n):
            nc.sync.dma_start(out=raws[n][:], in_=w2_rows[:, :, W2_LOADS[n][0] : W2_LOADS[n][1]])

        nc.vector.memset(tab_plane[:].bitcast(I32), 0)
        nc.gpsimd.memset(bias_rows[:], 0.0)
        nc.vector.memset(warm[:], 0.0)
        nc.vector.memset(w1_plane[:].bitcast(I32), 0)
        nc.vector.memset(w0_plane[:].bitcast(I32), 0)
        make_identity(nc, identity[:])

        nc.sync.dma_start(offsets[:], offs)
        nc.sync.dma_start(out=w1_codes[:], in_=w1_words[0].rearrange("p n i -> p (n i)").bitcast(I32))
        load_scale_rows(nc.sync, tab_plane, tab[0, K * T :].rearrange("(q t) -> q t", q=16), 0)
        nc.sync.dma_start(out=tab_words[:], in_=tab[0, 0 : K * T].rearrange("(p x) -> p x", p=P).bitcast(I32))
        nc.sync.dma_start(out=bias_rows[0:TILES, :], in_=b.rearrange("(m p) -> m p", p=P))
        nc.scalar.activation(out=warm_out[:], in_=warm[:], func=GELU)
        load_scale_rows(nc.sync, w1_plane, w1_scales[0], 4)
        nc.sync.dma_start(out=w0_codes[:].bitcast(I32), in_=w0_words[0].bitcast(I32))
        load_w2(0)
        load_scale_rows(nc.sync, w0_plane, w0_scales[0], 0)
        load_w2(1)
        load_w2(2)
        load_w2(3)

        turned = psum.tile([P, P], F32, name="turned", tag="acc%d" % (TILES - 1))
        nc.tensor.transpose(turned[:], bias_rows[:], identity[:])
        nc.scalar.copy(out=bias[:], in_=turned[:, 0:TILES])

        words, planes = {}, {}
        fields = [offsets[:, f * S // 16 : (f + 1) * S // 16] for f in range(3)]
        for kind, f in (("plane", 1), ("plane", 0), ("plane", 2), ("words", 1), ("words", 0), ("words", 2)):
            if kind == "plane":
                planes[f] = keep.tile([P, S], U8, name="plane%d" % f, align_bytes=64)
                nc.vector.tensor_copy(out=planes[f][:], in_=tab_plane[:].indirect(fields[f]))
            else:
                words[f] = keep.tile([P, S], U32, name="words%d" % f, align_bytes=64)
                nc.vector.tensor_copy(out=words[f][:], in_=tab_words[:].bitcast(U32).indirect(fields[f]))

        accs = [psum.tile([P, S], F32, name="acc%d" % m, tag="acc%d" % m) for m in range(TILES)]
        for m in range(TILES):
            nc.tensor.matmul_mx(
                out=accs[m][:],
                lhsT=w1_codes[:, m * P : (m + 1) * P].bitcast(FP8X4),
                lhsT_scale=w1_plane[4:P, m * P : (m + 1) * P],
                rhs=words[1][:].bitcast(FP8X4),
                rhs_scale=planes[1][:],
                start=True,
                stop=False,
            )

        w2_codes, w2_planes, grouped = {}, {}, {}

        def interleave(n):
            c0, c1, engine = W2_PARTS[n]
            load = [x for x, (l0, l1) in enumerate(W2_LOADS) if l0 <= c0 < l1][0]
            l0 = W2_LOADS[load][0]
            grouped[n] = keep.tile([P, c1 - c0, PACK], BF16, name="grouped%d" % n, align_bytes=64)
            dst = grouped[n][:].rearrange("p (c e) i -> p c i e", e=2)
            src = raws[load][:, :, c0 - l0 : c1 - l0].rearrange("p i (c e) -> p c i e", e=2)
            if engine == "scalar":
                nc.scalar.copy(out=dst, in_=src)
            else:
                nc.vector.tensor_copy(out=dst, in_=src)

        def quantize(n):
            c0, c1, engine = W2_PARTS[n]
            codes = keep.tile([P, c1 - c0], U32, name="w2_codes%d" % n, align_bytes=64)
            plane = keep.tile([P, c1 - c0], U8, name="w2_plane%d" % n, align_bytes=64)
            nc.vector.quantize_mx(
                out=codes[:].bitcast(FP8X4), scales=plane[:], in_=grouped[n][:].rearrange("p c i -> p (c i)")
            )
            for x in range((c1 - c0) // P):
                w2_codes[c0 // P + x] = codes[:, x * P : (x + 1) * P]
                w2_planes[c0 // P + x] = plane[:, x * P : (x + 1) * P]

        interleave(0)
        interleave(2)
        interleave(1)
        quantize(0)
        quantize(1)
        quantize(2)
        interleave(3)
        interleave(4)
        quantize(3)
        quantize(4)
        interleave(5)
        interleave(6)
        quantize(5)
        quantize(6)
        interleave(7)
        quantize(7)

        out_rows = out.rearrange("(m p) j -> p m j", p=P)
        for m0, m1 in STORES:
            result = keep.tile([P, m1 - m0, S], F32, name="result%d" % m0)
            for m in range(m0, m1):
                for h in range(S // P):
                    cols = slice(h * P, (h + 1) * P)
                    nc.tensor.matmul_mx(
                        out=accs[m][:, cols],
                        lhsT=w0_codes[:, 2 * m * P : 2 * (m + 1) * P].bitcast(FP4X4),
                        lhsT_scale=w0_plane[:, m * P : (m + 1) * P],
                        rhs=words[0][:, cols].bitcast(FP8X4),
                        rhs_scale=planes[0][:, cols],
                        start=False,
                        stop=False,
                    )
                nc.tensor.matmul_mx(
                    out=accs[m][:],
                    lhsT=w2_codes[m].bitcast(FP8X4),
                    lhsT_scale=w2_planes[m],
                    rhs=words[2][:].bitcast(FP8X4),
                    rhs_scale=planes[2][:],
                    start=False,
                    stop=True,
                )
                nc.scalar.activation(out=result[:, m - m0, :], in_=accs[m][:], func=GELU, bias=bias[:, m : m + 1])
            nc.sync.dma_start(out=out_rows[:, m0:m1, :], in_=result[:])
